import numpy as np
import ml_dtypes


def mxq(x, axis, fmt="e4m3"):
    dtype, down = {"e4m3": (ml_dtypes.float8_e4m3fn, 7), "e5m2": (ml_dtypes.float8_e5m2, 14)}[fmt]
    v = np.moveaxis(np.asarray(x, np.float32).astype(ml_dtypes.bfloat16).astype(np.float64), axis, -1)
    blocks = v.reshape(v.shape[:-1] + (-1, 32))
    amax = np.abs(blocks).max(-1, keepdims=True)
    byte = np.maximum(np.where(amax > 0, np.frexp(amax)[1] - 1 + 127, 0) - down, 1)
    scale = np.exp2(byte - 127.0)
    codes = (blocks / scale).astype(np.float32).astype(dtype).astype(np.float64)
    return np.moveaxis((codes * scale).reshape(v.shape), -1, axis)


WIDE = False


def mx_kscale(k):
    if not WIDE:
        return np.ones(k)
    levels = np.array([10, -10, 5, -5, 0])
    if k % 512:
        return np.exp2(np.random.permutation(np.resize(levels, k // 32))).repeat(32)
    a = np.empty((k // 512, 16))
    for p in range(k // 512):
        a[p, :8] = np.random.permutation(np.resize(levels, 8))
        for g in range(8):
            far = levels[np.abs(levels - a[p, g]) >= 10]
            a[p, g + 8] = far[np.random.randint(len(far))]
    return np.exp2(a.ravel()).repeat(32)


def f64(x):
    return np.asarray(x).astype(np.float64)


def striped(idx):
    return np.tile(np.asarray(idx).reshape(-1, 16).T, (8, 1)).astype(np.uint16)


def unstriped(offs):
    return offs[:16].T.reshape(-1).astype(np.int64)


E2M1 = np.array([0.0, 0.5, 1.0, 1.5, 2.0, 3.0, 4.0, 6.0, -0.0, -0.5, -1.0, -1.5, -2.0, -3.0, -4.0, -6.0])


def pack_weight(w, fmt):
    k, n = w.shape
    w = f64(np.asarray(w, np.float32).astype(ml_dtypes.bfloat16)).reshape(k // 32, 32, n)
    amax = np.abs(w).max(1)
    if fmt == "e4m3":
        byte = np.frexp(amax)[1] - 1 + 127 - 7
    else:
        mant, ex = np.frexp(amax / 6.0)
        byte = np.where(mant > 0.5, ex, ex - 1) + 127
    byte = np.clip(np.where(amax > 0, byte, 1), 1, 254)
    scaled = (w * np.exp2(127.0 - byte)[:, None, :]).reshape(k, n).astype(np.float32)
    by_word = np.ascontiguousarray(scaled.reshape(k // 512, 128, 4, n).transpose(0, 1, 3, 2))
    if fmt == "e4m3":
        words = by_word.astype(ml_dtypes.float8_e4m3fn).view(np.uint8)
    else:
        c = by_word.astype(ml_dtypes.float4_e2m1fn).view(np.uint8) & 0xF
        words = (c[..., 0::2] | (c[..., 1::2] << 4)).reshape(k // 512, 128, 2 * n)
    return np.ascontiguousarray(words), np.ascontiguousarray(byte.astype(np.uint8).reshape(k // 512, 16, n))


def unpack_weight(words, scales, fmt):
    g, _, n = scales.shape
    words = np.ascontiguousarray(words).reshape(g, 128, n, -1)
    if fmt == "e4m3":
        vals = words.view(ml_dtypes.float8_e4m3fn).astype(np.float64)
    else:
        nib = np.empty((g, 128, n, 4), np.uint8)
        nib[..., 0::2] = words & 0xF
        nib[..., 1::2] = words >> 4
        vals = E2M1[nib]
    vals = vals * np.repeat(np.exp2(scales.astype(np.float64) - 127.0), 8, axis=1)[..., None]
    return vals.transpose(0, 1, 3, 2).reshape(g * 512, n)


def bf(x):
    return np.asarray(x, np.float32).astype(ml_dtypes.bfloat16)


def planes(Y):
    r, m = Y.shape
    b = f64(bf(Y)).reshape(r // 32, 32, m)
    amax = np.abs(b).max(1)
    byte = np.clip(np.where(amax > 0, np.frexp(amax)[1] - 1 + 127 - 7, 1), 1, 254)
    codes = (b * np.exp2(127.0 - byte)[:, None, :]).reshape(r, m).astype(np.float32).astype(ml_dtypes.float8_e4m3fn).view(np.uint8)
    words = codes.reshape(r // 512, 128, 4, m).transpose(0, 1, 3, 2)
    return np.ascontiguousarray(words), np.ascontiguousarray(byte.astype(np.uint8).reshape(r // 512, 16, m))


K, L, T, J, N = 512, 512, 512, 256, 512


def setup_inputs():
    n = np.random.standard_normal
    idx = np.random.permutation(T)[:J]
    idx2 = np.random.permutation(T)[:J]
    fk = mx_kscale(K)
    fl = mx_kscale(L)
    xtp = pack_weight(n((K, T)) / fk[:, None], "e2m1")
    xsp = pack_weight(n((L, T)) / fl[:, None], "e4m3")
    wsp = pack_weight(n((L, N)) * 1 / np.sqrt(L) * fl[:, None], "e2m1")
    return {
        "xt_words": xtp[0],
        "xt_scales": xtp[1],
        "w": (n((K, N)) * 1 / np.sqrt(K) * fk[:, None]).astype(np.float32),
        "xs_words": xsp[0],
        "xs_scales": xsp[1],
        "ws_words": wsp[0],
        "ws_scales": wsp[1],
        "sh": (np.random.uniform(0.4, 1.0, (1, J))).astype(np.float32),
        "offs": striped(idx),
        "offs2": striped(idx2),
    }


def reference(xt_words, xt_scales, w, xs_words, xs_scales, ws_words, ws_scales, sh, offs, offs2):
    idx = unstriped(offs)
    idx2 = unstriped(offs2)
    xtu = unpack_weight(xt_words, xt_scales, "e2m1")
    xsu = unpack_weight(xs_words, xs_scales, "e4m3")
    wsu = unpack_weight(ws_words, ws_scales, "e2m1")
    wq = mxq(f64(w), 0, "e4m3")
    z = wq.T @ xtu
    s = wsu.T @ xsu
    d = f64(sh) * (z[:, idx2] - z[:, idx])
    p = np.zeros((N, T))
    p[:, idx] = d
    y = np.maximum(z + p, 0.0) + s
    words, scales = planes(y)
    return y, words, scales

@@ -1,0 +1,246 @@
+from contextlib import ExitStack
+
+import concourse.mybir as mybir
+from concourse.masks import make_identity
+
+K, L, T, J, N = 512, 512, 512, 256, 512
+FLOPS = 2 * K * N * T + 2 * L * N * T
+
+F32 = mybir.dt.float32
+BF16 = mybir.dt.bfloat16
+I32 = mybir.dt.int32
+U32 = mybir.dt.uint32
+U16 = mybir.dt.uint16
+U8 = mybir.dt.uint8
+FP8X4 = mybir.dt.float8_e4m3fn_x4
+FP4X4 = mybir.dt.float4_e2m1fn_x4
+ALU = mybir.AluOpType
+RELU = mybir.ActivationFunctionType.Relu
+
+P = 128
+PACK = 4
+HALF = 256
+
+
+def load_scale_plane(queue, plane, rows):
+    for q in range(4):
+        queue.dma_start(out=plane[32 * q : 32 * q + 4, :].bitcast(I32), in_=rows[0, 4 * q : 4 * q + 4, :].bitcast(I32))
+
+
+def tile_list_columns_toward_partners_pl_kernel(
+    tc, xt_words, xt_scales, w, xs_words, xs_scales, ws_words, ws_scales, sh, offs, offs2, out_0, out_1, out_2
+):
+    nc = tc.nc
+    with ExitStack() as ctx:
+        keep = ctx.enter_context(tc.tile_pool(name="keep", bufs=1))
+        psum = ctx.enter_context(tc.psum_pool(name="psum", bufs=1))
+
+        def bank(b):
+            return psum.tile([P, T], F32, name="bank%d" % b, tag="bank%d" % b)
+
+        xt_plane = keep.tile([P, T], U8, align_bytes=64)
+        xs_plane = keep.tile([P, T], U8, align_bytes=64)
+        ws_plane = keep.tile([P, N], U8, align_bytes=64)
+        nc.vector.memset(xt_plane[:].bitcast(U32), 0)
+
+        nc.vector.memset(ws_plane[:].bitcast(U32), 0)
+        nc.vector.memset(xs_plane[:].bitcast(U32), 0)
+        w_rows = w.rearrange("(p j) n -> p j n", j=PACK)
+        w_raw = [keep.tile([P, PACK, HALF], F32, name="w_raw%d" % h) for h in range(2)]
+        for h in range(2):
+            nc.sync.dma_start(out=w_raw[h][:], in_=w_rows[:, :, h * HALF : (h + 1) * HALF])
+        load_scale_plane(nc.scalar, xt_plane, xt_scales)
+        xt_codes = keep.tile([P, 2 * T], U8, align_bytes=64)
+        nc.sync.dma_start(out=xt_codes[:].bitcast(I32), in_=xt_words[0].bitcast(I32))
+        own = keep.tile([P, J // 16], U16)
+        partner = keep.tile([P, J // 16], U16)
+        nc.sync.dma_start(own[:], offs)
+        load_scale_plane(nc.gpsimd, ws_plane, ws_scales)
+        xs_codes = keep.tile([P, T], U32, align_bytes=64)
+        ws_codes = keep.tile([P, 2 * N], U8, align_bytes=64)
+        nc.sync.dma_start(partner[:], offs2)
+        share = keep.tile([P, J], F32)
+        nc.sync.dma_start(out=share[:], in_=sh[0].partition_broadcast(P))
+        nc.sync.dma_start(out=xs_codes[:].bitcast(I32), in_=xs_words[0].rearrange("p c r -> p (c r)").bitcast(I32))
+        nc.sync.dma_start(out=ws_codes[:].bitcast(I32), in_=ws_words[0].bitcast(I32))
+        load_scale_plane(nc.sync, xs_plane, xs_scales)
+
+        identity = keep.tile([P, P], F32)
+        make_identity(nc, identity[:])
+
+        placed = [keep.tile([P, T], F32, name="placed%d" % t) for t in range(PACK)]
+        for t in range(PACK):
+            nc.vector.memset(placed[t][:], 0.0)
+
+        w_bf = keep.tile([P, PACK, P, PACK], BF16, align_bytes=64)
+        m_half = P // 2
+
+        def round_w(h, t0, t1):
+            nc.vector.tensor_copy(
+                out=w_bf[:, t0:t1, h * m_half : (h + 1) * m_half, :].rearrange("p t m j -> p m t j"),
+                in_=w_raw[h][:].rearrange("p j (m t) -> p m t j", t=PACK)[:, :, t0:t1, :],
+            )
+
+        w_codes = keep.tile([P, N], U32, align_bytes=64)
+        w_plane = keep.tile([P, N], U8, align_bytes=64)
+
+        def quantise_w(t0, t1):
+            nc.vector.quantize_mx(
+                out=w_codes[:, t0 * P : t1 * P].bitcast(FP8X4),
+                scales=w_plane[:, t0 * P : t1 * P],
+                in_=w_bf[:, t0:t1, :, :].rearrange("p t m j -> p (t m j)"),
+            )
+
+        z = [keep.tile([P, T], F32, name="z%d" % t) for t in range(PACK)]
+
+        def make_z(t, c0, c1, b):
+            acc = bank(b)
+            nc.tensor.matmul_mx(
+                out=acc[:, c0:c1],
+                lhsT=w_codes[:, t * P : (t + 1) * P].bitcast(FP8X4),
+                lhsT_scale=w_plane[:, t * P : (t + 1) * P],
+                rhs=xt_codes[:, 2 * c0 : 2 * c1].bitcast(FP4X4),
+                rhs_scale=xt_plane[:, c0:c1],
+                start=True,
+                stop=True,
+            )
+            nc.scalar.copy(out=z[t][:, c0:c1], in_=acc[:, c0:c1])
+
+        round_w(0, 0, PACK)
+        round_w(1, 0, 1)
+        quantise_w(0, 1)
+        make_z(0, 0, HALF, 0)
+        make_z(0, HALF, T, 1)
+        round_w(1, 1, PACK)
+        quantise_w(1, 2)
+        make_z(1, 0, T, 2)
+        quantise_w(2, 4)
+        make_z(2, 0, T, 3)
+        make_z(3, 0, T, 0)
+
+        s_tok = keep.tile([P, PACK, PACK, P], F32)
+        for b in range(PACK):
+            acc = bank(4 + b)
+            nc.tensor.matmul_mx(
+                out=acc[:],
+                lhsT=xs_codes[:, b * P : (b + 1) * P].bitcast(FP8X4),
+                lhsT_scale=xs_plane[:, b * P : (b + 1) * P],
+                rhs=ws_codes[:].bitcast(FP4X4),
+                rhs_scale=ws_plane[:],
+                start=True,
+                stop=True,
+            )
+            nc.scalar.copy(out=s_tok[:, b, :, :], in_=acc[:].rearrange("p (m t) -> p t m", t=PACK))
+
+        total = [bank((t + 1) % PACK) for t in range(PACK)]
+
+        def turn_s_block(b):
+            for t in range(PACK):
+                nc.tensor.matmul(
+                    total[t][:, b * P : (b + 1) * P],
+                    lhsT=s_tok[:, b, t, :],
+                    rhs=identity[:],
+                    is_transpose=True,
+                    start=(b == 0),
+                    stop=(t == PACK - 1 and b == PACK - 1),
+                )
+
+        turn_s_block(0)
+        turn_s_block(1)
+
+        def turn_into(acc, blocks, start, stop):
+            for b in range(PACK):
+                nc.tensor.matmul(
+                    acc[:, b * P : (b + 1) * P],
+                    lhsT=blocks[b],
+                    rhs=identity[:],
+                    is_transpose=True,
+                    start=(start and b == 0),
+                    stop=(stop and b == PACK - 1),
+                )
+
+        def blocks_of(tile):
+            return [tile[:, b * P : (b + 1) * P] for b in range(PACK)]
+
+        gap = [keep.tile([P, J], F32, name="gap%d" % t) for t in range(PACK)]
+        mine = [keep.tile([P, J], F32, name="mine%d" % t) for t in range(2)] + gap[0:2]
+
+        def gather_own(t):
+            nc.vector.tensor_copy(out=mine[t][:], in_=z[t][:].indirect(own[:]))
+
+        def gather_gap(t):
+            nc.vector.tensor_tensor(gap[t][:], z[t][:].indirect(partner[:]), mine[t][:], ALU.subtract)
+
+        def scatter(t):
+            nc.vector.tensor_tensor(placed[t][:].indirect(own[:]), gap[t][:], share[:], ALU.mult)
+
+        y = keep.tile([P, PACK, T], F32)
+        out_rows = out_0.rearrange("(p t) c -> p t c", t=PACK)
+        last = PACK - 1
+
+        moved = [bank(5), bank(6)]
+
+        def finish_on_tensor(t):
+            if t == 0:
+                turn_into(moved[0], blocks_of(z[0]), True, False)
+            turn_into(moved[t], blocks_of(placed[t]), False, True)
+            if t == 0:
+                turn_s_block(2)
+                turn_s_block(3)
+                turn_into(moved[1], blocks_of(z[1]), True, False)
+            r_tok = keep.tile([P, T], F32, name="r_tok%d" % t)
+            nc.scalar.activation(out=r_tok[:], in_=moved[t][:], func=RELU)
+            turn_into(total[t], blocks_of(r_tok), False, True)
+            nc.scalar.copy(out=y[:, t, :], in_=total[t][:])
+            if t == 0:
+                moved.append(bank(1))
+            if t == 1:
+                turn_into(moved[2], blocks_of(z[2]), True, False)
+            if t < 2:
+                nc.sync.dma_start(out=out_rows[:, t, :], in_=y[:, t, :])
+
+        y_bf = keep.tile([P, T, PACK], BF16, align_bytes=64)
+
+        def weave(c0, c1, t0):
+            return dict(out=y_bf[:, c0:c1, t0 : t0 + 2], in_=y[:, t0 : t0 + 2, c0:c1].rearrange("p t c -> p c t"))
+
+        gather_own(0)
+        gather_gap(0)
+        for t in range(PACK):
+            if t < last:
+                gather_own(t + 1)
+            scatter(t)
+            if t < last:
+                gather_gap(t + 1)
+                finish_on_tensor(t)
+            if t == 1:
+                nc.scalar.copy(**weave(0, T, 0))
+
+        s_last = total[last]
+        moved_last = keep.tile([P, T], F32)
+        for h in range(2):
+            cols = slice(h * HALF, (h + 1) * HALF)
+            nc.vector.tensor_tensor(moved_last[:, cols], z[last][:, cols], placed[last][:, cols], ALU.add)
+        for h in range(2):
+            cols = slice(h * HALF, (h + 1) * HALF)
+            nc.vector.scalar_tensor_tensor(
+                out=y[:, last, cols], in0=moved_last[:, cols], scalar=0.0, in1=s_last[:, cols], op0=ALU.max, op1=ALU.add
+            )
+        nc.sync.dma_start(out=out_rows[:, 2:4, :], in_=y[:, 2:4, :])
+
+        nc.scalar.copy(**weave(0, HALF, 2))
+        nc.vector.tensor_copy(**weave(HALF, T, 2))
+        y_codes = keep.tile([P, T], U32, align_bytes=64)
+        y_plane = keep.tile([P, T], U8, align_bytes=64)
+        out_words = out_1[0].rearrange("p c r -> p (c r)").bitcast(I32)
+        for h in (1, 0):
+            cols = slice(h * HALF, (h + 1) * HALF)
+            nc.vector.quantize_mx(
+                out=y_codes[:, cols].bitcast(FP8X4),
+                scales=y_plane[:, cols],
+                in_=y_bf[:, cols, :].rearrange("p c t -> p (c t)"),
+            )
+            nc.sync.dma_start(out=out_words[:, cols], in_=y_codes[:, cols].bitcast(I32))
+        for q in range(4):
+            queue = nc.scalar if q % 2 == 0 else nc.sync
+            queue.dma_start(out=out_2[0, 4 * q : 4 * q + 4, :].bitcast(I32), in_=y_plane[32 * q : 32 * q + 4, :].bitcast(I32))

@@ -38,12 +38,15 @@ def tile_list_columns_toward_partners_pl_kernel(
         def bank(b):
             return psum.tile([P, T], F32, name="bank%d" % b, tag="bank%d" % b)
 
+        identity = keep.tile([P, P], F32)
+        make_identity(nc, identity[:])
         xt_plane = keep.tile([P, T], U8, align_bytes=64)
         xs_plane = keep.tile([P, T], U8, align_bytes=64)
         ws_plane = keep.tile([P, N], U8, align_bytes=64)
         nc.vector.memset(xt_plane[:].bitcast(U32), 0)
+        nc.gpsimd.memset(ws_plane[:].bitcast(U32), 0)
+        load_scale_plane(nc.gpsimd, ws_plane, ws_scales)
 
-        nc.vector.memset(ws_plane[:].bitcast(U32), 0)
         nc.vector.memset(xs_plane[:].bitcast(U32), 0)
         w_rows = w.rearrange("(p j) n -> p j n", j=PACK)
         w_raw = [keep.tile([P, PACK, HALF], F32, name="w_raw%d" % h) for h in range(2)]
@@ -55,18 +58,16 @@ def tile_list_columns_toward_partners_pl_kernel(
         own = keep.tile([P, J // 16], U16)
         partner = keep.tile([P, J // 16], U16)
         nc.sync.dma_start(own[:], offs)
-        load_scale_plane(nc.gpsimd, ws_plane, ws_scales)
         xs_codes = keep.tile([P, T], U32, align_bytes=64)
         ws_codes = keep.tile([P, 2 * N], U8, align_bytes=64)
         nc.sync.dma_start(partner[:], offs2)
-        share = keep.tile([P, J], F32)
-        nc.sync.dma_start(out=share[:], in_=sh[0].partition_broadcast(P))
+        sh_row = keep.tile([P, J], F32)
+        nc.vector.memset(sh_row[:], 0.0)
+        nc.sync.dma_start(out=sh_row[0:1, :], in_=sh)
         nc.sync.dma_start(out=xs_codes[:].bitcast(I32), in_=xs_words[0].rearrange("p c r -> p (c r)").bitcast(I32))
         nc.sync.dma_start(out=ws_codes[:].bitcast(I32), in_=ws_words[0].bitcast(I32))
         load_scale_plane(nc.sync, xs_plane, xs_scales)
 
-        identity = keep.tile([P, P], F32)
-        make_identity(nc, identity[:])
 
         placed = [keep.tile([P, T], F32, name="placed%d" % t) for t in range(PACK)]
         for t in range(PACK):
@@ -115,6 +116,16 @@ def tile_list_columns_toward_partners_pl_kernel(
         quantise_w(1, 2)
         make_z(1, 0, T, 2)
         quantise_w(2, 4)
+        sh_turned = bank(6)
+        for c in range(2):
+            nc.tensor.transpose(sh_turned[:, c * P : (c + 1) * P], sh_row[:, c * P : (c + 1) * P], identity[:])
+        sh_cols = keep.tile([P, 2], F32)
+        nc.scalar.copy(out=sh_cols[:], in_=sh_turned[:, 0:J:P])
+        sh_spread = bank(7)
+        for c in range(2):
+            nc.tensor.transpose(sh_spread[:, c * P : (c + 1) * P], sh_cols[:, c : c + 1].to_broadcast([P, P]), identity[:])
+        share = keep.tile([P, J], F32)
+        nc.scalar.copy(out=share[:], in_=sh_spread[:, 0:J])
         make_z(2, 0, T, 3)
         make_z(3, 0, T, 0)
 
@@ -142,7 +153,7 @@ def tile_list_columns_toward_partners_pl_kernel(
                     rhs=identity[:],
                     is_transpose=True,
                     start=(b == 0),
-                    stop=(t == PACK - 1 and b == PACK - 1),
+                    stop=(t >= 2 and b == PACK - 1),
                 )
 
         turn_s_block(0)
@@ -188,16 +199,19 @@ def tile_list_columns_toward_partners_pl_kernel(
                 turn_s_block(2)
                 turn_s_block(3)
                 turn_into(moved[1], blocks_of(z[1]), True, False)
-            r_tok = keep.tile([P, T], F32, name="r_tok%d" % t)
+            r_tok = keep.tile([P, T], F32, name="r_tok%d" % t, tag="r_tok%d" % t)
             nc.scalar.activation(out=r_tok[:], in_=moved[t][:], func=RELU)
             turn_into(total[t], blocks_of(r_tok), False, True)
             nc.scalar.copy(out=y[:, t, :], in_=total[t][:])
-            if t == 0:
-                moved.append(bank(1))
-            if t == 1:
-                turn_into(moved[2], blocks_of(z[2]), True, False)
-            if t < 2:
-                nc.sync.dma_start(out=out_rows[:, t, :], in_=y[:, t, :])
+            nc.sync.dma_start(out=out_rows[:, t, :], in_=y[:, t, :])
+
+        def add_placed(summed, t, cols):
+            nc.vector.tensor_tensor(summed[:, t - 2, cols], z[t][:, cols], placed[t][:, cols], ALU.add)
+
+        def relu_plus_s(summed, t, cols):
+            nc.vector.scalar_tensor_tensor(
+                out=y[:, t, cols], in0=summed[:, t - 2, cols], scalar=0.0, in1=total[t][:, cols], op0=ALU.max, op1=ALU.add
+            )
 
         y_bf = keep.tile([P, T, PACK], BF16, align_bytes=64)
 
@@ -206,28 +220,29 @@ def tile_list_columns_toward_partners_pl_kernel(
 
         gather_own(0)
         gather_gap(0)
-        for t in range(PACK):
-            if t < last:
-                gather_own(t + 1)
-            scatter(t)
-            if t < last:
-                gather_gap(t + 1)
-                finish_on_tensor(t)
-            if t == 1:
-                nc.scalar.copy(**weave(0, T, 0))
-
-        s_last = total[last]
-        moved_last = keep.tile([P, T], F32)
-        for h in range(2):
-            cols = slice(h * HALF, (h + 1) * HALF)
-            nc.vector.tensor_tensor(moved_last[:, cols], z[last][:, cols], placed[last][:, cols], ALU.add)
-        for h in range(2):
-            cols = slice(h * HALF, (h + 1) * HALF)
-            nc.vector.scalar_tensor_tensor(
-                out=y[:, last, cols], in0=moved_last[:, cols], scalar=0.0, in1=s_last[:, cols], op0=ALU.max, op1=ALU.add
-            )
-        nc.sync.dma_start(out=out_rows[:, 2:4, :], in_=y[:, 2:4, :])
-
+        gather_own(1)
+        scatter(0)
+        finish_on_tensor(0)
+        gather_gap(1)
+        gather_own(2)
+        scatter(1)
+        finish_on_tensor(1)
+        nc.scalar.copy(**weave(0, T, 0))
+        gather_gap(2)
+        gather_own(3)
+        scatter(2)
+        gather_gap(3)
+        summed = keep.tile([P, 2, T], F32, name="summed", tag="r_tok1")
+        add_placed(summed, 2, slice(0, T))
+        scatter(3)
+        relu_plus_s(summed, 2, slice(0, T))
+        nc.sync.dma_start(out=out_rows[:, 2, :], in_=y[:, 2, :])
+        halves = [slice(0, HALF), slice(HALF, T)]
+        for cols in halves:
+            add_placed(summed, 3, cols)
+        for cols in halves:
+            relu_plus_s(summed, 3, cols)
+        nc.sync.dma_start(out=out_rows[:, 3, :], in_=y[:, 3, :])
         nc.scalar.copy(**weave(0, HALF, 2))
         nc.vector.tensor_copy(**weave(HALF, T, 2))
         y_codes = keep.tile([P, T], U32, align_bytes=64)

@@ -76,8 +76,8 @@ def tile_list_columns_toward_partners_pl_kernel(
         w_bf = keep.tile([P, PACK, P, PACK], BF16, align_bytes=64)
         m_half = P // 2
 
-        def round_w(h, t0, t1):
-            nc.vector.tensor_copy(
+        def round_w(copy, h, t0, t1):
+            copy(
                 out=w_bf[:, t0:t1, h * m_half : (h + 1) * m_half, :].rearrange("p t m j -> p m t j"),
                 in_=w_raw[h][:].rearrange("p j (m t) -> p m t j", t=PACK)[:, :, t0:t1, :],
             )
@@ -107,12 +107,14 @@ def tile_list_columns_toward_partners_pl_kernel(
             )
             nc.scalar.copy(out=z[t][:, c0:c1], in_=acc[:, c0:c1])
 
-        round_w(0, 0, PACK)
-        round_w(1, 0, 1)
+        round_w(nc.vector.tensor_copy, 0, 0, 3)
+        round_w(nc.scalar.copy, 0, 3, 4)
+        round_w(nc.vector.tensor_copy, 1, 0, 1)
+        round_w(nc.scalar.copy, 1, 3, 4)
         quantise_w(0, 1)
         make_z(0, 0, HALF, 0)
         make_z(0, HALF, T, 1)
-        round_w(1, 1, PACK)
+        round_w(nc.vector.tensor_copy, 1, 1, 3)
         quantise_w(1, 2)
         make_z(1, 0, T, 2)
         quantise_w(2, 4)
@@ -145,8 +147,8 @@ def tile_list_columns_toward_partners_pl_kernel(
 
         total = [bank((t + 1) % PACK) for t in range(PACK)]
 
-        def turn_s_block(b):
-            for t in range(PACK):
+        def turn_s_block(b, slices):
+            for t in slices:
                 nc.tensor.matmul(
                     total[t][:, b * P : (b + 1) * P],
                     lhsT=s_tok[:, b, t, :],
@@ -156,8 +158,8 @@ def tile_list_columns_toward_partners_pl_kernel(
                     stop=(t >= 2 and b == PACK - 1),
                 )
 
-        turn_s_block(0)
-        turn_s_block(1)
+        turn_s_block(0, (0, 1))
+        turn_s_block(1, (0, 1))
 
         def turn_into(acc, blocks, start, stop):
             for b in range(PACK):
@@ -196,8 +198,8 @@ def tile_list_columns_toward_partners_pl_kernel(
                 turn_into(moved[0], blocks_of(z[0]), True, False)
             turn_into(moved[t], blocks_of(placed[t]), False, True)
             if t == 0:
-                turn_s_block(2)
-                turn_s_block(3)
+                turn_s_block(2, (0, 1))
+                turn_s_block(3, (0, 1))
                 turn_into(moved[1], blocks_of(z[1]), True, False)
             r_tok = keep.tile([P, T], F32, name="r_tok%d" % t, tag="r_tok%d" % t)
             nc.scalar.activation(out=r_tok[:], in_=moved[t][:], func=RELU)
@@ -228,6 +230,8 @@ def tile_list_columns_toward_partners_pl_kernel(
         scatter(1)
         finish_on_tensor(1)
         nc.scalar.copy(**weave(0, T, 0))
+        for b in range(PACK):
+            turn_s_block(b, (2, 3))
         gather_gap(2)
         gather_own(3)
         scatter(2)
@@ -248,7 +252,7 @@ def tile_list_columns_toward_partners_pl_kernel(
         y_codes = keep.tile([P, T], U32, align_bytes=64)
         y_plane = keep.tile([P, T], U8, align_bytes=64)
         out_words = out_1[0].rearrange("p c r -> p (c r)").bitcast(I32)
-        for h in (1, 0):
+        for h in range(2):
             cols = slice(h * HALF, (h + 1) * HALF)
             nc.vector.quantize_mx(
                 out=y_codes[:, cols].bitcast(FP8X4),

from contextlib import ExitStack

import concourse.mybir as mybir
from concourse.masks import make_identity

K, L, T, J, N = 512, 512, 512, 256, 512
FLOPS = 2 * K * N * T + 2 * L * N * T

F32 = mybir.dt.float32
BF16 = mybir.dt.bfloat16
I32 = mybir.dt.int32
U32 = mybir.dt.uint32
U16 = mybir.dt.uint16
U8 = mybir.dt.uint8
FP8X4 = mybir.dt.float8_e4m3fn_x4
FP4X4 = mybir.dt.float4_e2m1fn_x4
ALU = mybir.AluOpType
RELU = mybir.ActivationFunctionType.Relu

P = 128
PACK = 4
HALF = 256


def load_scale_plane(queue, plane, rows):
    for q in range(4):
        queue.dma_start(out=plane[32 * q : 32 * q + 4, :].bitcast(I32), in_=rows[0, 4 * q : 4 * q + 4, :].bitcast(I32))


def tile_list_columns_toward_partners_pl_kernel(
    tc, xt_words, xt_scales, w, xs_words, xs_scales, ws_words, ws_scales, sh, offs, offs2, out_0, out_1, out_2
):
    nc = tc.nc
    with ExitStack() as ctx:
        keep = ctx.enter_context(tc.tile_pool(name="keep", bufs=1))
        psum = ctx.enter_context(tc.psum_pool(name="psum", bufs=1))

        def bank(b):
            return psum.tile([P, T], F32, name="bank%d" % b, tag="bank%d" % b)

        identity = keep.tile([P, P], F32)
        make_identity(nc, identity[:])
        xt_plane = keep.tile([P, T], U8, align_bytes=64)
        xs_plane = keep.tile([P, T], U8, align_bytes=64)
        ws_plane = keep.tile([P, N], U8, align_bytes=64)
        nc.vector.memset(xt_plane[:].bitcast(U32), 0)
        nc.gpsimd.memset(ws_plane[:].bitcast(U32), 0)
        load_scale_plane(nc.gpsimd, ws_plane, ws_scales)

        nc.vector.memset(xs_plane[:].bitcast(U32), 0)
        w_rows = w.rearrange("(p j) n -> p j n", j=PACK)
        w_raw = [keep.tile([P, PACK, HALF], F32, name="w_raw%d" % h) for h in range(2)]
        for h in range(2):
            nc.sync.dma_start(out=w_raw[h][:], in_=w_rows[:, :, h * HALF : (h + 1) * HALF])
        load_scale_plane(nc.scalar, xt_plane, xt_scales)
        xt_codes = keep.tile([P, 2 * T], U8, align_bytes=64)
        nc.sync.dma_start(out=xt_codes[:].bitcast(I32), in_=xt_words[0].bitcast(I32))
        own = keep.tile([P, J // 16], U16)
        partner = keep.tile([P, J // 16], U16)
        nc.sync.dma_start(own[:], offs)
        xs_codes = keep.tile([P, T], U32, align_bytes=64)
        ws_codes = keep.tile([P, 2 * N], U8, align_bytes=64)
        nc.sync.dma_start(partner[:], offs2)
        sh_row = keep.tile([P, J], F32)
        nc.vector.memset(sh_row[:], 0.0)
        nc.sync.dma_start(out=sh_row[0:1, :], in_=sh)
        nc.sync.dma_start(out=xs_codes[:].bitcast(I32), in_=xs_words[0].rearrange("p c r -> p (c r)").bitcast(I32))
        nc.sync.dma_start(out=ws_codes[:].bitcast(I32), in_=ws_words[0].bitcast(I32))
        load_scale_plane(nc.sync, xs_plane, xs_scales)


        placed = [keep.tile([P, T], F32, name="placed%d" % t) for t in range(PACK)]
        for t in range(PACK):
            nc.vector.memset(placed[t][:], 0.0)

        w_bf = keep.tile([P, PACK, P, PACK], BF16, align_bytes=64)
        m_half = P // 2

        def round_w(copy, h, t0, t1):
            copy(
                out=w_bf[:, t0:t1, h * m_half : (h + 1) * m_half, :].rearrange("p t m j -> p m t j"),
                in_=w_raw[h][:].rearrange("p j (m t) -> p m t j", t=PACK)[:, :, t0:t1, :],
            )

        w_codes = keep.tile([P, N], U32, align_bytes=64)
        w_plane = keep.tile([P, N], U8, align_bytes=64)

        def quantise_w(t0, t1):
            nc.vector.quantize_mx(
                out=w_codes[:, t0 * P : t1 * P].bitcast(FP8X4),
                scales=w_plane[:, t0 * P : t1 * P],
                in_=w_bf[:, t0:t1, :, :].rearrange("p t m j -> p (t m j)"),
            )

        z = [keep.tile([P, T], F32, name="z%d" % t) for t in range(PACK)]

        def make_z(t, c0, c1, b):
            acc = bank(b)
            nc.tensor.matmul_mx(
                out=acc[:, c0:c1],
                lhsT=w_codes[:, t * P : (t + 1) * P].bitcast(FP8X4),
                lhsT_scale=w_plane[:, t * P : (t + 1) * P],
                rhs=xt_codes[:, 2 * c0 : 2 * c1].bitcast(FP4X4),
                rhs_scale=xt_plane[:, c0:c1],
                start=True,
                stop=True,
            )
            nc.scalar.copy(out=z[t][:, c0:c1], in_=acc[:, c0:c1])

        round_w(nc.vector.tensor_copy, 0, 0, 3)
        round_w(nc.scalar.copy, 0, 3, 4)
        round_w(nc.vector.tensor_copy, 1, 0, 1)
        round_w(nc.scalar.copy, 1, 3, 4)
        quantise_w(0, 1)
        make_z(0, 0, HALF, 0)
        make_z(0, HALF, T, 1)
        round_w(nc.vector.tensor_copy, 1, 1, 3)
        quantise_w(1, 2)
        make_z(1, 0, T, 2)
        quantise_w(2, 4)
        sh_turned = bank(6)
        for c in range(2):
            nc.tensor.transpose(sh_turned[:, c * P : (c + 1) * P], sh_row[:, c * P : (c + 1) * P], identity[:])
        sh_cols = keep.tile([P, 2], F32)
        nc.scalar.copy(out=sh_cols[:], in_=sh_turned[:, 0:J:P])
        sh_spread = bank(7)
        for c in range(2):
            nc.tensor.transpose(sh_spread[:, c * P : (c + 1) * P], sh_cols[:, c : c + 1].to_broadcast([P, P]), identity[:])
        share = keep.tile([P, J], F32)
        nc.scalar.copy(out=share[:], in_=sh_spread[:, 0:J])
        make_z(2, 0, T, 3)
        make_z(3, 0, T, 0)

        s_tok = keep.tile([P, PACK, PACK, P], F32)
        for b in range(PACK):
            acc = bank(4 + b)
            nc.tensor.matmul_mx(
                out=acc[:],
                lhsT=xs_codes[:, b * P : (b + 1) * P].bitcast(FP8X4),
                lhsT_scale=xs_plane[:, b * P : (b + 1) * P],
                rhs=ws_codes[:].bitcast(FP4X4),
                rhs_scale=ws_plane[:],
                start=True,
                stop=True,
            )
            nc.scalar.copy(out=s_tok[:, b, :, :], in_=acc[:].rearrange("p (m t) -> p t m", t=PACK))

        total = [bank((t + 1) % PACK) for t in range(PACK)]

        def turn_s_block(b, slices):
            for t in slices:
                nc.tensor.matmul(
                    total[t][:, b * P : (b + 1) * P],
                    lhsT=s_tok[:, b, t, :],
                    rhs=identity[:],
                    is_transpose=True,
                    start=(b == 0),
                    stop=(t >= 2 and b == PACK - 1),
                )

        turn_s_block(0, (0, 1))
        turn_s_block(1, (0, 1))

        def turn_into(acc, blocks, start, stop):
            for b in range(PACK):
                nc.tensor.matmul(
                    acc[:, b * P : (b + 1) * P],
                    lhsT=blocks[b],
                    rhs=identity[:],
                    is_transpose=True,
                    start=(start and b == 0),
                    stop=(stop and b == PACK - 1),
                )

        def blocks_of(tile):
            return [tile[:, b * P : (b + 1) * P] for b in range(PACK)]

        gap = [keep.tile([P, J], F32, name="gap%d" % t) for t in range(PACK)]
        mine = [keep.tile([P, J], F32, name="mine%d" % t) for t in range(2)] + gap[0:2]

        def gather_own(t):
            nc.vector.tensor_copy(out=mine[t][:], in_=z[t][:].indirect(own[:]))

        def gather_gap(t):
            nc.vector.tensor_tensor(gap[t][:], z[t][:].indirect(partner[:]), mine[t][:], ALU.subtract)

        def scatter(t):
            nc.vector.tensor_tensor(placed[t][:].indirect(own[:]), gap[t][:], share[:], ALU.mult)

        y = keep.tile([P, PACK, T], F32)
        out_rows = out_0.rearrange("(p t) c -> p t c", t=PACK)
        last = PACK - 1

        moved = [bank(5), bank(6)]

        def finish_on_tensor(t):
            if t == 0:
                turn_into(moved[0], blocks_of(z[0]), True, False)
            turn_into(moved[t], blocks_of(placed[t]), False, True)
            if t == 0:
                turn_s_block(2, (0, 1))
                turn_s_block(3, (0, 1))
                turn_into(moved[1], blocks_of(z[1]), True, False)
            r_tok = keep.tile([P, T], F32, name="r_tok%d" % t, tag="r_tok%d" % t)
            nc.scalar.activation(out=r_tok[:], in_=moved[t][:], func=RELU)
            turn_into(total[t], blocks_of(r_tok), False, True)
            nc.scalar.copy(out=y[:, t, :], in_=total[t][:])
            nc.sync.dma_start(out=out_rows[:, t, :], in_=y[:, t, :])

        def add_placed(summed, t, cols):
            nc.vector.tensor_tensor(summed[:, t - 2, cols], z[t][:, cols], placed[t][:, cols], ALU.add)

        def relu_plus_s(summed, t, cols):
            nc.vector.scalar_tensor_tensor(
                out=y[:, t, cols], in0=summed[:, t - 2, cols], scalar=0.0, in1=total[t][:, cols], op0=ALU.max, op1=ALU.add
            )

        y_bf = keep.tile([P, T, PACK], BF16, align_bytes=64)

        def weave(c0, c1, t0):
            return dict(out=y_bf[:, c0:c1, t0 : t0 + 2], in_=y[:, t0 : t0 + 2, c0:c1].rearrange("p t c -> p c t"))

        gather_own(0)
        gather_gap(0)
        gather_own(1)
        scatter(0)
        finish_on_tensor(0)
        gather_gap(1)
        gather_own(2)
        scatter(1)
        finish_on_tensor(1)
        nc.scalar.copy(**weave(0, T, 0))
        for b in range(PACK):
            turn_s_block(b, (2, 3))
        gather_gap(2)
        gather_own(3)
        scatter(2)
        gather_gap(3)
        summed = keep.tile([P, 2, T], F32, name="summed", tag="r_tok1")
        add_placed(summed, 2, slice(0, T))
        scatter(3)
        relu_plus_s(summed, 2, slice(0, T))
        nc.sync.dma_start(out=out_rows[:, 2, :], in_=y[:, 2, :])
        halves = [slice(0, HALF), slice(HALF, T)]
        for cols in halves:
            add_placed(summed, 3, cols)
        for cols in halves:
            relu_plus_s(summed, 3, cols)
        nc.sync.dma_start(out=out_rows[:, 3, :], in_=y[:, 3, :])
        nc.scalar.copy(**weave(0, HALF, 2))
        nc.vector.tensor_copy(**weave(HALF, T, 2))
        y_codes = keep.tile([P, T], U32, align_bytes=64)
        y_plane = keep.tile([P, T], U8, align_bytes=64)
        out_words = out_1[0].rearrange("p c r -> p (c r)").bitcast(I32)
        for h in range(2):
            cols = slice(h * HALF, (h + 1) * HALF)
            nc.vector.quantize_mx(
                out=y_codes[:, cols].bitcast(FP8X4),
                scales=y_plane[:, cols],
                in_=y_bf[:, cols, :].rearrange("p c t -> p (c t)"),
            )
            nc.sync.dma_start(out=out_words[:, cols], in_=y_codes[:, cols].bitcast(I32))
        for q in range(4):
            queue = nc.scalar if q % 2 == 0 else nc.sync
            queue.dma_start(out=out_2[0, 4 * q : 4 * q + 4, :].bitcast(I32), in_=y_plane[32 * q : 32 * q + 4, :].bitcast(I32))
